import numpy as np
import ml_dtypes


def mxq(x, axis, fmt="e4m3"):
    dtype, down = {"e4m3": (ml_dtypes.float8_e4m3fn, 7), "e5m2": (ml_dtypes.float8_e5m2, 14)}[fmt]
    v = np.moveaxis(np.asarray(x, np.float32).astype(ml_dtypes.bfloat16).astype(np.float64), axis, -1)
    blocks = v.reshape(v.shape[:-1] + (-1, 32))
    amax = np.abs(blocks).max(-1, keepdims=True)
    byte = np.maximum(np.where(amax > 0, np.frexp(amax)[1] - 1 + 127, 0) - down, 1)
    scale = np.exp2(byte - 127.0)
    codes = (blocks / scale).astype(np.float32).astype(dtype).astype(np.float64)
    return np.moveaxis((codes * scale).reshape(v.shape), -1, axis)


WIDE = False


def mx_kscale(k):
    if not WIDE:
        return np.ones(k)
    levels = np.array([10, -10, 5, -5, 0])
    if k % 512:
        return np.exp2(np.random.permutation(np.resize(levels, k // 32))).repeat(32)
    a = np.empty((k // 512, 16))
    for p in range(k // 512):
        a[p, :8] = np.random.permutation(np.resize(levels, 8))
        for g in range(8):
            far = levels[np.abs(levels - a[p, g]) >= 10]
            a[p, g + 8] = far[np.random.randint(len(far))]
    return np.exp2(a.ravel()).repeat(32)


def f64(x):
    return np.asarray(x).astype(np.float64)


def striped(idx):
    return np.tile(idx.reshape(-1, 16).T, (8, 1)).astype(np.uint16)


def unstriped(offs):
    return offs[:16].T.reshape(-1).astype(np.int64)


def striped8(idx):
    return np.concatenate([x.reshape(-1, 16).T for x in idx]).astype(np.uint16)


def runs(offs, k):
    lists = np.stack([offs[16 * r : 16 * r + 16].T.reshape(-1) for r in range(8)]).astype(np.int64)
    return lists[np.arange(k) % 512 // 64]


def pack_weight(w):
    k, n = w.shape
    w = f64(np.asarray(w, np.float32).astype(ml_dtypes.bfloat16)).reshape(k // 32, 32, n)
    amax = np.abs(w).max(1)
    byte = np.clip(np.where(amax > 0, np.frexp(amax)[1] - 1 + 127 - 7, 1), 1, 254)
    scaled = (w * np.exp2(127.0 - byte)[:, None, :]).reshape(k, n).astype(np.float32)
    words = np.ascontiguousarray(scaled.reshape(k // 512, 128, 4, n).transpose(0, 1, 3, 2)).astype(ml_dtypes.float8_e4m3fn).view(np.uint8)
    return words, np.ascontiguousarray(byte.astype(np.uint8).reshape(k // 512, 16, n))


def unpack_weight(words, scales):
    g, p, n, _ = words.shape
    vals = np.ascontiguousarray(words).view(ml_dtypes.float8_e4m3fn).astype(np.float64) * np.repeat(np.exp2(scales.astype(np.float64) - 127.0), 8, axis=1)[..., None]
    return vals.transpose(0, 1, 3, 2).reshape(g * 512, n)

def planes(y):
    n, m = y.shape
    v = y.astype(np.float32).astype(ml_dtypes.bfloat16).astype(np.float64).reshape(n // 32, 32, m)
    top = np.abs(v).max(1)
    byte = np.clip(np.where(top > 0, np.frexp(top)[1] - 1 + 127 - 7, 1), 1, 254)
    codes = (v * np.exp2(127.0 - byte)[:, None, :]).reshape(n, m).astype(np.float32).astype(ml_dtypes.float8_e4m3fn).view(np.uint8)
    words = codes.reshape(n // 512, 128, 4, m).transpose(0, 1, 3, 2)
    return np.ascontiguousarray(words), np.ascontiguousarray(byte.astype(np.uint8).reshape(n // 512, 16, m))


K, T, S, N, H, G = 512, 1024, 512, 512, 512, 2048


def setup_inputs():
    n = np.random.standard_normal
    s = mx_kscale(K)[:, None]
    u = mx_kscale(S)
    packed_xT = pack_weight(n((K, T)) * s)
    packed_w1 = pack_weight(n((K, H)) / np.sqrt(K) / s)
    packed_dT = pack_weight(n((K, G)) / s)
    packed_w2 = pack_weight(n((H, N)) / np.sqrt(2 * H) / u[:, None])
    packed_w3 = pack_weight(n((H, N)) / np.sqrt(2 * H) / u[:, None])
    return {
        "x_words": packed_xT[0],
        "x_scales": packed_xT[1],
        "w1_words": packed_w1[0],
        "w1_scales": packed_w1[1],
        "d_words": packed_dT[0],
        "d_scales": packed_dT[1],
        "gn": (np.random.uniform(0.5, 1.5, (H, 1)) * u[:, None]).astype(np.float32),
        "gk": (np.random.uniform(0.5, 1.5, (H, 1)) * u[:, None]).astype(np.float32),
        "w2_words": packed_w2[0],
        "w2_scales": packed_w2[1],
        "w3_words": packed_w3[0],
        "w3_scales": packed_w3[1],
        "offs": striped(np.random.permutation(T)[:S]),
        "kidx": striped8(np.random.randint(0, G, (8, H))),
        "two": striped(np.random.permutation(T)[:S]),
        "n1": striped8(np.stack([np.random.permutation(S) for _ in range(8)])),
        "n2": striped(np.random.permutation(S)),
        "n3": striped(np.random.permutation(S)),
        "n4": striped(np.random.permutation(S)),
        "n5": striped(np.random.permutation(S)),
    }


def reference(x_words, x_scales, w1_words, w1_scales, d_words, d_scales, gn, gk, w2_words, w2_scales, w3_words, w3_scales, offs, kidx, two, n1, n2, n3, n4, n5):
    xq = unpack_weight(x_words, x_scales)[:, unstriped(offs)]
    y = unpack_weight(w1_words, w1_scales).T @ xq
    st = y - (y[np.arange(H)[:, None], runs(n1, H)])
    z = f64(gn) * (st - (0.5 * (st[np.arange(H)[:, None], runs(n1, H)])))
    d_kidx = unpack_weight(d_words, d_scales)[np.arange(K)[:, None], runs(kidx, K)]
    x_two = unpack_weight(x_words, x_scales)[:, unstriped(two)]
    s = 0.0625 * (d_kidx.T @ x_two)
    st2 = s + s[:, unstriped(n2)]
    z2 = f64(gk) * (st2 * (np.tanh(st2[:, unstriped(n3)])))
    h = unpack_weight(w2_words, w2_scales).T @ mxq(z, 0, "e4m3") + unpack_weight(w3_words, w3_scales).T @ mxq(z2, 0, "e4m3")
    st3 = np.maximum(h, h[:, unstriped(n4)])
    out_0 = st3[:, unstriped(n5)] - (0.5 * h)
    return (out_0,) + planes(out_0)

@@ -1,0 +1,243 @@
+from contextlib import ExitStack
+
+import concourse.mybir as mybir
+
+K, T, S, N, H, G = 512, 1024, 512, 512, 512, 2048
+FLOPS = 4 * 2 * 512 * 512 * 512
+
+F32 = mybir.dt.float32
+BF16 = mybir.dt.bfloat16
+I32 = mybir.dt.int32
+U32 = mybir.dt.uint32
+U16 = mybir.dt.uint16
+U8 = mybir.dt.uint8
+FP8X4 = mybir.dt.float8_e4m3fn_x4
+ALU = mybir.AluOpType
+ACT = mybir.ActivationFunctionType
+
+P = 128
+PACK = 4
+HALF = S // 2
+LIST_COLS = S // 16
+
+
+def tile_picked_jkeytwicehopphopb_none_po_kernel(
+    tc, x_words, x_scales, w1_words, w1_scales, d_words, d_scales, gn, gk, w2_words, w2_scales, w3_words, w3_scales,
+    offs, kidx, two, n1, n2, n3, n4, n5, out_0, out_1, out_2,
+):
+    nc = tc.nc
+    planes = range(PACK)
+    halves = range(2)
+
+    with ExitStack() as ctx:
+        lists = ctx.enter_context(tc.tile_pool(name="lists", bufs=1))
+        sb = ctx.enter_context(tc.tile_pool(name="sb", bufs=1))
+        psum = ctx.enter_context(tc.psum_pool(name="psum", bufs=1))
+
+        def tile(name, shape, dtype):
+            return sb.tile(shape, dtype, name=name, align_bytes=64)
+
+        def load_list(name, src):
+            dst = lists.tile([P, LIST_COLS], U16, name=name)
+            nc.sync.dma_start(dst[:], src)
+            return dst
+
+        def load_words(name, src):
+            dst = tile(name, [P, src.shape[2]], I32)
+            nc.sync.dma_start(dst[:], src[0].rearrange("p n t -> p (n t)").bitcast(I32))
+            return dst
+
+        def load_scales_repeated(name, src):
+            dst = tile(name, [P, src.shape[2]], U8)
+            for q in range(4):
+                rows = src[0, 4 * q : 4 * q + 4, :].bitcast(I32).rearrange("r c -> (r c)")
+                nc.sync.dma_start(dst[32 * q : 32 * q + 32, :].bitcast(I32), rows.partition_broadcast(8))
+            return dst
+
+        def load_gain(name, src):
+            dst = tile(name, [P, PACK], F32)
+            nc.sync.dma_start(dst[:], src.rearrange("(p t) o -> p (t o)", t=PACK))
+            return dst
+
+        def deal(name, src, dtype):
+            dst = tile(name, [P, 512], dtype)
+            nc.vector.tensor_copy(dst[:].rearrange("p (t m) -> p m t", t=PACK), src.rearrange("p (m t) -> p m t", t=PACK))
+            return dst
+
+        def pick_words(name, table, offsets):
+            dst = tile(name, [P, 512], I32)
+            nc.vector.tensor_copy(dst[:].bitcast(U32), table[:].bitcast(U32).indirect(offsets[:]))
+            return dst
+
+        def pick_scales(name, table, offsets):
+            dst = tile(name, [P, 512], U8)
+            nc.vector.tensor_copy(dst[:], table[:].indirect(offsets[:]))
+            return dst
+
+        def cols(h):
+            return slice(h * HALF, (h + 1) * HALF)
+
+        def fetch(on_vector, dst, window, offsets, h):
+            looked_up = window[:].indirect(offsets[:, h * LIST_COLS // 2 : (h + 1) * LIST_COLS // 2])
+            if on_vector:
+                nc.vector.tensor_copy(dst, looked_up)
+            else:
+                nc.scalar.activation(dst, looked_up, ACT.Copy)
+
+        def mx(out, w_words, w_scales, t, a_words, a_scales, start, stop):
+            m = slice(t * P, (t + 1) * P)
+            nc.tensor.matmul_mx(
+                out, lhsT=w_words[:, m].bitcast(FP8X4), lhsT_scale=w_scales[:, m],
+                rhs=a_words.bitcast(FP8X4), rhs_scale=a_scales, start=start, stop=stop,
+            )
+
+        def quantise(name, src, words, scales):
+            woven = tile(name, [P, HALF, PACK], BF16)
+            nc.vector.tensor_copy(
+                woven[:].rearrange("p (c i) t -> p c t i", i=4), src[:].rearrange("p t (c i) -> p c t i", i=4)
+            )
+            nc.vector.quantize_mx(words.bitcast(FP8X4), scales, woven[:].rearrange("p j t -> p (j t)"))
+
+        d_scale_table = tile("d_scale_table", [P, G], U8)
+        nc.gpsimd.memset(d_scale_table[:].bitcast(I32), 0)
+        key_scales = tile("key_scales", [P, H], U8)
+        nc.gpsimd.memset(key_scales[:].bitcast(I32), 0)
+        w23_scales_raw = tile("w23_scales_raw", [P, N], U8)
+        nc.gpsimd.memset(w23_scales_raw[:].bitcast(I32), 0)
+
+        offs_l = load_list("offs_l", offs)
+        x_scale_table = load_scales_repeated("x_scale_table", x_scales)
+        x_table = load_words("x_table", x_words)
+        w1_raw = load_words("w1_raw", w1_words)
+        w1_scales_raw = load_scales_repeated("w1_scales_raw", w1_scales)
+        kidx_l = load_list("kidx_l", kidx)
+        nc.sync.dma_start(d_scale_table[0:P:8, :].bitcast(I32), d_scales[0].bitcast(I32))
+        gn_t = load_gain("gn_t", gn)
+        n1_l = load_list("n1_l", n1)
+        two_l = load_list("two_l", two)
+        d_table = load_words("d_table", d_words)
+        n2_l = load_list("n2_l", n2)
+        gk_t = load_gain("gk_t", gk)
+        n3_l = load_list("n3_l", n3)
+        w2_raw = load_words("w2_raw", w2_words)
+        w3_raw = load_words("w3_raw", w3_words)
+        for k, src in ((0, w2_scales), (4, w3_scales)):
+            for q in range(4):
+                nc.sync.dma_start(
+                    w23_scales_raw[32 * q + k : 32 * q + k + 4, :].bitcast(I32), src[0, 4 * q : 4 * q + 4, :].bitcast(I32)
+                )
+        n4_l = load_list("n4_l", n4)
+        n5_l = load_list("n5_l", n5)
+
+        w1 = deal("w1", w1_raw[:], I32)
+        xq_scales = pick_scales("xq_scales", x_scale_table, offs_l)
+        xq_words = pick_words("xq_words", x_table, offs_l)
+        w1_s = deal("w1_s", w1_scales_raw[:], U8)
+        y_banks = [psum.tile([P, S], F32, name="y%d" % t, tag="bank%d" % t) for t in planes]
+        for t in planes:
+            mx(y_banks[t][:], w1, w1_s, t, xq_words[:], xq_scales[:], True, True)
+
+        key_scales_picked = pick_scales("key_scales_picked", d_scale_table, kidx_l)
+        key_scales_dealt = deal("key_scales_dealt", key_scales_picked[:], U8)
+        for r in range(4):
+            nc.sync.dma_start(key_scales[r:P:32, :].bitcast(I32), key_scales_dealt[8 * r : P : 32, :].bitcast(I32))
+        x2_scales = pick_scales("x2_scales", x_scale_table, two_l)
+        x2_words = pick_words("x2_words", x_table, two_l)
+        keys_picked = pick_words("keys_picked", d_table, kidx_l)
+        keys = deal("keys", keys_picked[:], I32)
+        s_banks = [psum.tile([P, S], F32, name="s%d" % t, tag="bank%d" % (PACK + t)) for t in planes]
+        for t in planes:
+            mx(s_banks[t][:], keys, key_scales, t, x2_words[:], x2_scales[:], True, True)
+
+        st = []
+        for t in planes:
+            y = tile("y_sb%d" % t, [P, S], F32)
+            nc.scalar.activation(y[:], y_banks[t][:], ACT.Copy, scale=gn_t[:, t : t + 1])
+            far = tile("y_far%d" % t, [P, S], F32)
+            for h in halves:
+                fetch(False, far[:, cols(h)], y, n1_l, h)
+            st.append(tile("st%d" % t, [P, S], F32))
+            nc.vector.tensor_tensor(st[t][:], y[:], far[:], ALU.subtract)
+
+        w2 = deal("w2", w2_raw[:], I32)
+        w3 = deal("w3", w3_raw[:], I32)
+        w23_s = deal("w23_s", w23_scales_raw[:], U8)
+
+        z_planes = [tile("z_planes%d" % h, [P, PACK, HALF], BF16) for h in halves]
+        st2 = []
+        for t in planes:
+            s = tile("s_sb%d" % t, [P, S], F32)
+            nc.scalar.activation(s[:], s_banks[t][:], ACT.Copy, scale=0.0625)
+            far = tile("s_far%d" % t, [P, S], F32)
+            for h in halves:
+                fetch(False, far[:, cols(h)], s, n2_l, h)
+            far2 = tile("st_far%d" % t, [P, S], F32)
+            for h in halves:
+                fetch(True, far2[:, cols(h)], st[t], n1_l, h)
+            for h in halves:
+                nc.vector.scalar_tensor_tensor(
+                    z_planes[h][:, t, :], far2[:, cols(h)], -0.5, st[t][:, cols(h)], ALU.mult, ALU.add
+                )
+            st2.append(tile("st2_%d" % t, [P, S], F32))
+            nc.vector.tensor_tensor(st2[t][:], s[:], far[:], ALU.add)
+
+        h_banks = [
+            [psum.tile([P, HALF], F32, name="h%d_%d" % (h, t), tag="bank%d" % (PACK * h + t)) for t in planes]
+            for h in halves
+        ]
+        for h in halves:
+            z_words = tile("z_words%d" % h, [P, HALF], U32)
+            z_scales = tile("z_scales%d" % h, [P, HALF], U8)
+            quantise("z_woven%d" % h, z_planes[h], z_words[:], z_scales[:])
+            for t in planes:
+                mx(h_banks[h][t][:], w2, w23_s, t, z_words[:], z_scales[:], True, False)
+
+        th = []
+        for t in planes:
+            th.append(tile("tanh%d" % t, [P, S], F32))
+            nc.scalar.activation(th[t][:], st2[t][:], ACT.Tanh)
+        hs = [tile("h_sb%d" % t, [P, S], F32) for t in planes]
+        for h in halves:
+            z2_planes = tile("z2_planes%d" % h, [P, PACK, HALF], BF16)
+            for t in planes:
+                far = tile("tanh_far%d_%d" % (h, t), [P, HALF], F32)
+                fetch(False, far[:], th[t], n3_l, h)
+                nc.vector.scalar_tensor_tensor(
+                    z2_planes[:, t, :], st2[t][:, cols(h)], gk_t[:, t : t + 1], far[:], ALU.mult, ALU.mult
+                )
+            z2_words = tile("z2_words%d" % h, [P, HALF], U32)
+            z2_scales = tile("z2_scales%d" % h, [P, HALF], U8)
+            quantise("z2_woven%d" % h, z2_planes, z2_words[:], z2_scales[:])
+            for t in planes:
+                mx(h_banks[h][t][:], w3, w23_s[4:P, :], t, z2_words[:], z2_scales[:], False, True)
+        for h in halves:
+            for t in planes:
+                if h == 1 and t % 2 == 1:
+                    nc.vector.tensor_copy(hs[t][:, cols(h)], h_banks[h][t][:])
+                else:
+                    nc.scalar.copy(hs[t][:, cols(h)], h_banks[h][t][:])
+
+        st3 = []
+        for t in planes:
+            far = tile("h_far%d" % t, [P, S], F32)
+            for h in halves:
+                fetch(t == 1, far[:, cols(h)], hs[t], n4_l, h)
+            st3.append(tile("st3_%d" % t, [P, S], F32))
+            nc.vector.tensor_tensor(st3[t][:], hs[t][:], far[:], ALU.max)
+
+        out_rows = out_0.rearrange("(p t) j -> p t j", t=PACK)
+        out_word_rows = out_1[0].rearrange("p n t -> p (n t)").bitcast(I32)
+        out_scales = tile("out_scales", [P, S], U8)
+        for h in halves:
+            res = tile("res%d" % h, [P, PACK, HALF], F32)
+            for t in planes:
+                far = tile("st3_far%d_%d" % (h, t), [P, HALF], F32)
+                fetch(t == 0, far[:], st3[t], n5_l, h)
+                nc.vector.scalar_tensor_tensor(res[:, t, :], hs[t][:, cols(h)], -0.5, far[:], ALU.mult, ALU.add)
+            nc.sync.dma_start(out_rows[:, :, cols(h)], res[:])
+            out_words = tile("out_words%d" % h, [P, HALF], I32)
+            quantise("out_woven%d" % h, res, out_words[:], out_scales[:, cols(h)])
+            nc.sync.dma_start(out_word_rows[:, cols(h)], out_words[:])
+        for q in range(4):
+            queue = nc.scalar if q % 2 else nc.sync
+            queue.dma_start(out_2[0, 4 * q : 4 * q + 4, :].bitcast(I32), out_scales[32 * q : 32 * q + 4, :].bitcast(I32))

@@ -19,6 +19,17 @@ P = 128
 PACK = 4
 HALF = S // 2
 LIST_COLS = S // 16
+HALVES = [(0, HALF), (HALF, S)]
+Z2_CHUNKS = [(0, 256), (256, S)]
+OUT_CHUNKS = [(0, 256), (256, S)]
+PIECES = [(0, HALF)]
+LAG = 1
+V_N1A = ()
+V_N2 = ()
+V_N1B = (0, 1, 2, 3)
+V_N3 = ()
+V_N4 = (1, 3)
+V_N5 = ((0, 0),)
 
 
 def tile_picked_jkeytwicehopphopb_none_po_kernel(
@@ -27,15 +38,15 @@ def tile_picked_jkeytwicehopphopb_none_po_kernel(
 ):
     nc = tc.nc
     planes = range(PACK)
-    halves = range(2)
 
     with ExitStack() as ctx:
         lists = ctx.enter_context(tc.tile_pool(name="lists", bufs=1))
         sb = ctx.enter_context(tc.tile_pool(name="sb", bufs=1))
+        reused = ctx.enter_context(tc.tile_pool(name="reused", bufs=1))
         psum = ctx.enter_context(tc.psum_pool(name="psum", bufs=1))
 
-        def tile(name, shape, dtype):
-            return sb.tile(shape, dtype, name=name, align_bytes=64)
+        def tile(name, shape, dtype, tag=None):
+            return sb.tile(shape, dtype, name=name, tag=tag or name, align_bytes=64)
 
         def load_list(name, src):
             dst = lists.tile([P, LIST_COLS], U16, name=name)
@@ -74,11 +85,8 @@ def tile_picked_jkeytwicehopphopb_none_po_kernel(
             nc.vector.tensor_copy(dst[:], table[:].indirect(offsets[:]))
             return dst
 
-        def cols(h):
-            return slice(h * HALF, (h + 1) * HALF)
-
-        def fetch(on_vector, dst, window, offsets, h):
-            looked_up = window[:].indirect(offsets[:, h * LIST_COLS // 2 : (h + 1) * LIST_COLS // 2])
+        def fetch(on_vector, dst, window, offsets, lo, hi):
+            looked_up = window[:].indirect(offsets[:, lo // 16 : hi // 16])
             if on_vector:
                 nc.vector.tensor_copy(dst, looked_up)
             else:
@@ -92,7 +100,7 @@ def tile_picked_jkeytwicehopphopb_none_po_kernel(
             )
 
         def quantise(name, src, words, scales):
-            woven = tile(name, [P, HALF, PACK], BF16)
+            woven = tile(name, [P, src.shape[2], PACK], BF16)
             nc.vector.tensor_copy(
                 woven[:].rearrange("p (c i) t -> p c t i", i=4), src[:].rearrange("p t (c i) -> p c t i", i=4)
             )
@@ -102,8 +110,6 @@ def tile_picked_jkeytwicehopphopb_none_po_kernel(
         nc.gpsimd.memset(d_scale_table[:].bitcast(I32), 0)
         key_scales = tile("key_scales", [P, H], U8)
         nc.gpsimd.memset(key_scales[:].bitcast(I32), 0)
-        w23_scales_raw = tile("w23_scales_raw", [P, N], U8)
-        nc.gpsimd.memset(w23_scales_raw[:].bitcast(I32), 0)
 
         offs_l = load_list("offs_l", offs)
         x_scale_table = load_scales_repeated("x_scale_table", x_scales)
@@ -115,19 +121,9 @@ def tile_picked_jkeytwicehopphopb_none_po_kernel(
         gn_t = load_gain("gn_t", gn)
         n1_l = load_list("n1_l", n1)
         two_l = load_list("two_l", two)
-        d_table = load_words("d_table", d_words)
+        d_table = reused.tile([P, G], I32, name="d_table", offset=0)
+        nc.sync.dma_start(d_table[:], d_words[0].rearrange("p n t -> p (n t)").bitcast(I32))
         n2_l = load_list("n2_l", n2)
-        gk_t = load_gain("gk_t", gk)
-        n3_l = load_list("n3_l", n3)
-        w2_raw = load_words("w2_raw", w2_words)
-        w3_raw = load_words("w3_raw", w3_words)
-        for k, src in ((0, w2_scales), (4, w3_scales)):
-            for q in range(4):
-                nc.sync.dma_start(
-                    w23_scales_raw[32 * q + k : 32 * q + k + 4, :].bitcast(I32), src[0, 4 * q : 4 * q + 4, :].bitcast(I32)
-                )
-        n4_l = load_list("n4_l", n4)
-        n5_l = load_list("n5_l", n5)
 
         w1 = deal("w1", w1_raw[:], I32)
         xq_scales = pick_scales("xq_scales", x_scale_table, offs_l)
@@ -141,6 +137,19 @@ def tile_picked_jkeytwicehopphopb_none_po_kernel(
         key_scales_dealt = deal("key_scales_dealt", key_scales_picked[:], U8)
         for r in range(4):
             nc.sync.dma_start(key_scales[r:P:32, :].bitcast(I32), key_scales_dealt[8 * r : P : 32, :].bitcast(I32))
+        w23_scales_raw = tile("w23_scales_raw", [P, N], U8, tag="key_scales_picked")
+        nc.gpsimd.memset(w23_scales_raw[:].bitcast(I32), 0)
+        w2_raw = load_words("w2_raw", w2_words)
+        w3_raw = load_words("w3_raw", w3_words)
+        for k, src in ((0, w2_scales), (4, w3_scales)):
+            for q in range(4):
+                nc.sync.dma_start(
+                    w23_scales_raw[32 * q + k : 32 * q + k + 4, :].bitcast(I32), src[0, 4 * q : 4 * q + 4, :].bitcast(I32)
+                )
+        gk_t = load_gain("gk_t", gk)
+        n3_l = load_list("n3_l", n3)
+        n4_l = load_list("n4_l", n4)
+        n5_l = load_list("n5_l", n5)
         x2_scales = pick_scales("x2_scales", x_scale_table, two_l)
         x2_words = pick_words("x2_words", x_table, two_l)
         keys_picked = pick_words("keys_picked", d_table, kidx_l)
@@ -149,95 +158,103 @@ def tile_picked_jkeytwicehopphopb_none_po_kernel(
         for t in planes:
             mx(s_banks[t][:], keys, key_scales, t, x2_words[:], x2_scales[:], True, True)
 
+        z_planes = tile("z_planes", [P, PACK, S], BF16)
         st = []
+
+        def z_second_hop(t):
+            far = tile("st_far%d" % t, [P, S], F32)
+            for lo, hi in HALVES:
+                fetch(t in V_N1B, far[:, lo:hi], st[t], n1_l, lo, hi)
+            nc.vector.scalar_tensor_tensor(z_planes[:, t, :], far[:], -0.5, st[t][:], ALU.mult, ALU.add)
+
         for t in planes:
             y = tile("y_sb%d" % t, [P, S], F32)
             nc.scalar.activation(y[:], y_banks[t][:], ACT.Copy, scale=gn_t[:, t : t + 1])
             far = tile("y_far%d" % t, [P, S], F32)
-            for h in halves:
-                fetch(False, far[:, cols(h)], y, n1_l, h)
-            st.append(tile("st%d" % t, [P, S], F32))
+            for lo, hi in HALVES:
+                fetch(t in V_N1A, far[:, lo:hi], y, n1_l, lo, hi)
+            st.append(reused.tile([P, S], F32, name="st%d" % t, offset=4 * S * t))
             nc.vector.tensor_tensor(st[t][:], y[:], far[:], ALU.subtract)
+            if t >= LAG:
+                z_second_hop(t - LAG)
 
         w2 = deal("w2", w2_raw[:], I32)
         w3 = deal("w3", w3_raw[:], I32)
         w23_s = deal("w23_s", w23_scales_raw[:], U8)
 
-        z_planes = [tile("z_planes%d" % h, [P, PACK, HALF], BF16) for h in halves]
         st2 = []
+        th = []
         for t in planes:
             s = tile("s_sb%d" % t, [P, S], F32)
             nc.scalar.activation(s[:], s_banks[t][:], ACT.Copy, scale=0.0625)
             far = tile("s_far%d" % t, [P, S], F32)
-            for h in halves:
-                fetch(False, far[:, cols(h)], s, n2_l, h)
-            far2 = tile("st_far%d" % t, [P, S], F32)
-            for h in halves:
-                fetch(True, far2[:, cols(h)], st[t], n1_l, h)
-            for h in halves:
-                nc.vector.scalar_tensor_tensor(
-                    z_planes[h][:, t, :], far2[:, cols(h)], -0.5, st[t][:, cols(h)], ALU.mult, ALU.add
-                )
+            for lo, hi in HALVES:
+                fetch(t in V_N2, far[:, lo:hi], s, n2_l, lo, hi)
             st2.append(tile("st2_%d" % t, [P, S], F32))
             nc.vector.tensor_tensor(st2[t][:], s[:], far[:], ALU.add)
-
-        h_banks = [
-            [psum.tile([P, HALF], F32, name="h%d_%d" % (h, t), tag="bank%d" % (PACK * h + t)) for t in planes]
-            for h in halves
-        ]
-        for h in halves:
-            z_words = tile("z_words%d" % h, [P, HALF], U32)
-            z_scales = tile("z_scales%d" % h, [P, HALF], U8)
-            quantise("z_woven%d" % h, z_planes[h], z_words[:], z_scales[:])
-            for t in planes:
-                mx(h_banks[h][t][:], w2, w23_s, t, z_words[:], z_scales[:], True, False)
-
-        th = []
-        for t in planes:
             th.append(tile("tanh%d" % t, [P, S], F32))
             nc.scalar.activation(th[t][:], st2[t][:], ACT.Tanh)
+            if t < LAG:
+                z_second_hop(PACK - LAG + t)
+
+        z_words = tile("z_words", [P, S], U32)
+        z_scales = tile("z_scales", [P, S], U8)
+        quantise("z_woven", z_planes, z_words[:], z_scales[:])
+
         hs = [tile("h_sb%d" % t, [P, S], F32) for t in planes]
-        for h in halves:
-            z2_planes = tile("z2_planes%d" % h, [P, PACK, HALF], BF16)
+        h_banks = [
+            [psum.tile([P, hi - lo], F32, name="h%d_%d" % (c, t), tag="bank%d" % (PACK * c + t)) for t in planes]
+            for c, (lo, hi) in enumerate(Z2_CHUNKS)
+        ]
+        lo, hi = Z2_CHUNKS[1]
+        for t in planes:
+            mx(h_banks[1][t][:], w2, w23_s, t, z_words[:, lo:hi], z_scales[:, lo:hi], True, False)
+        for c, (lo, hi) in enumerate(Z2_CHUNKS):
+            z2_planes = tile("z2_planes%d" % c, [P, PACK, hi - lo], BF16)
             for t in planes:
-                far = tile("tanh_far%d_%d" % (h, t), [P, HALF], F32)
-                fetch(False, far[:], th[t], n3_l, h)
+                far = tile("tanh_far%d_%d" % (c, t), [P, hi - lo], F32)
+                fetch((c, t) in V_N3, far[:], th[t], n3_l, lo, hi)
                 nc.vector.scalar_tensor_tensor(
-                    z2_planes[:, t, :], st2[t][:, cols(h)], gk_t[:, t : t + 1], far[:], ALU.mult, ALU.mult
+                    z2_planes[:, t, :], st2[t][:, lo:hi], gk_t[:, t : t + 1], far[:], ALU.mult, ALU.mult
                 )
-            z2_words = tile("z2_words%d" % h, [P, HALF], U32)
-            z2_scales = tile("z2_scales%d" % h, [P, HALF], U8)
-            quantise("z2_woven%d" % h, z2_planes, z2_words[:], z2_scales[:])
+            z2_words = tile("z2_words%d" % c, [P, hi - lo], U32)
+            z2_scales = tile("z2_scales%d" % c, [P, hi - lo], U8)
+            quantise("z2_woven%d" % c, z2_planes, z2_words[:], z2_scales[:])
             for t in planes:
-                mx(h_banks[h][t][:], w3, w23_s[4:P, :], t, z2_words[:], z2_scales[:], False, True)
-        for h in halves:
-            for t in planes:
-                if h == 1 and t % 2 == 1:
-                    nc.vector.tensor_copy(hs[t][:, cols(h)], h_banks[h][t][:])
+                if c == 1:
+                    mx(h_banks[c][t][:], w3, w23_s[4:P, :], t, z2_words[:], z2_scales[:], False, True)
                 else:
-                    nc.scalar.copy(hs[t][:, cols(h)], h_banks[h][t][:])
+                    for a, b in PIECES:
+                        mx(h_banks[c][t][:, a:b], w2, w23_s, t, z_words[:, a:b], z_scales[:, a:b], True, False)
+                        mx(h_banks[c][t][:, a:b], w3, w23_s[4:P, :], t, z2_words[:, a:b], z2_scales[:, a:b], False, True)
+        for c, (lo, hi) in enumerate(Z2_CHUNKS):
+            for t in planes:
+                if c == 1 and t % 2 == 1:
+                    nc.vector.tensor_copy(hs[t][:, lo:hi], h_banks[c][t][:])
+                else:
+                    nc.scalar.copy(hs[t][:, lo:hi], h_banks[c][t][:])
 
         st3 = []
         for t in planes:
             far = tile("h_far%d" % t, [P, S], F32)
-            for h in halves:
-                fetch(t == 1, far[:, cols(h)], hs[t], n4_l, h)
+            for lo, hi in HALVES:
+                fetch(t in V_N4, far[:, lo:hi], hs[t], n4_l, lo, hi)
             st3.append(tile("st3_%d" % t, [P, S], F32))
             nc.vector.tensor_tensor(st3[t][:], hs[t][:], far[:], ALU.max)
 
         out_rows = out_0.rearrange("(p t) j -> p t j", t=PACK)
         out_word_rows = out_1[0].rearrange("p n t -> p (n t)").bitcast(I32)
         out_scales = tile("out_scales", [P, S], U8)
-        for h in halves:
-            res = tile("res%d" % h, [P, PACK, HALF], F32)
+        for c, (lo, hi) in enumerate(OUT_CHUNKS):
+            res = tile("res%d" % c, [P, PACK, hi - lo], F32)
             for t in planes:
-                far = tile("st3_far%d_%d" % (h, t), [P, HALF], F32)
-                fetch(t == 0, far[:], st3[t], n5_l, h)
-                nc.vector.scalar_tensor_tensor(res[:, t, :], hs[t][:, cols(h)], -0.5, far[:], ALU.mult, ALU.add)
-            nc.sync.dma_start(out_rows[:, :, cols(h)], res[:])
-            out_words = tile("out_words%d" % h, [P, HALF], I32)
-            quantise("out_woven%d" % h, res, out_words[:], out_scales[:, cols(h)])
-            nc.sync.dma_start(out_word_rows[:, cols(h)], out_words[:])
+                far = tile("st3_far%d_%d" % (c, t), [P, hi - lo], F32)
+                fetch((c, t) in V_N5, far[:], st3[t], n5_l, lo, hi)
+                nc.vector.scalar_tensor_tensor(res[:, t, :], hs[t][:, lo:hi], -0.5, far[:], ALU.mult, ALU.add)
+            nc.sync.dma_start(out_rows[:, :, lo:hi], res[:])
+            out_words = tile("out_words%d" % c, [P, hi - lo], I32)
+            quantise("out_woven%d" % c, res, out_words[:], out_scales[:, lo:hi])
+            nc.sync.dma_start(out_word_rows[:, lo:hi], out_words[:])
         for q in range(4):
             queue = nc.scalar if q % 2 else nc.sync
             queue.dma_start(out_2[0, 4 * q : 4 * q + 4, :].bitcast(I32), out_scales[32 * q : 32 * q + 4, :].bitcast(I32))

@@ -23,13 +23,28 @@ HALVES = [(0, HALF), (HALF, S)]
 Z2_CHUNKS = [(0, 256), (256, S)]
 OUT_CHUNKS = [(0, 256), (256, S)]
 PIECES = [(0, HALF)]
+P_SUB = (0, 1, 2, 3)
+P_ADD = ()
+P_DEAL = False
+P_RES = ()
+ZOFF = 45
+RING3 = 8
+RING5 = 8
+SOFF = 0
+ORDER = "ye.0 yh.0 sub.0 ye.1 yh.1 sub.1 ye.2 yh.2 sub.2 zh.0 ye.3 yh.3 sub.3 zh.1 zh.2 deal se.0 sh.0 add.0 zh.3 zc.0 se.1 sh.1 add.1 zc.1 se.2 sh.2 add.2 zc.2 se.3 sh.3 add.3 zc.3 th.0 th.1 th.2 th.3 zq g3.0.0 g3.1.0 g3.2.0 g3.3.0 z2q.0.0 g3.0.1 g3.1.1 g3.2.1 g3.3.1 z2q.0.1"
+HOLD3 = True
+HOLD5 = True
+SUBHOLD = 1
+P_W1 = False
+ZH = (0, 1, 2, None)
+V_EV = ((1, 1), (1, 3))
 LAG = 1
-V_N1A = ()
+V_N1A = (2,)
 V_N2 = ()
 V_N1B = (0, 1, 2, 3)
 V_N3 = ()
-V_N4 = (1, 3)
-V_N5 = ((0, 0),)
+V_N4 = ((0,1),(1,1),(0,3))
+V_N5 = ((0,0),)
 
 
 def tile_picked_jkeytwicehopphopb_none_po_kernel(
@@ -70,13 +85,22 @@ def tile_picked_jkeytwicehopphopb_none_po_kernel(
             nc.sync.dma_start(dst[:], src.rearrange("(p t) o -> p (t o)", t=PACK))
             return dst
 
-        def deal(name, src, dtype):
-            dst = tile(name, [P, 512], dtype)
+        def deal(name, src, dtype, on_pool=False, offset=None):
+            if offset is None:
+                dst = tile(name, [P, 512], dtype)
+            else:
+                dst = reused.tile([P, 512], dtype, name=name, offset=offset, align_bytes=64)
+            if on_pool:
+                nc.gpsimd.tensor_copy(dst[:].rearrange("p (t m) -> p t m", t=PACK), src.rearrange("p (m t) -> p t m", t=PACK))
+                return dst
             nc.vector.tensor_copy(dst[:].rearrange("p (t m) -> p m t", t=PACK), src.rearrange("p (m t) -> p m t", t=PACK))
             return dst
 
-        def pick_words(name, table, offsets):
-            dst = tile(name, [P, 512], I32)
+        def pick_words(name, table, offsets, offset=None):
+            if offset is None:
+                dst = tile(name, [P, 512], I32)
+            else:
+                dst = reused.tile([P, 512], I32, name=name, offset=offset)
             nc.vector.tensor_copy(dst[:].bitcast(U32), table[:].bitcast(U32).indirect(offsets[:]))
             return dst
 
@@ -125,7 +149,7 @@ def tile_picked_jkeytwicehopphopb_none_po_kernel(
         nc.sync.dma_start(d_table[:], d_words[0].rearrange("p n t -> p (n t)").bitcast(I32))
         n2_l = load_list("n2_l", n2)
 
-        w1 = deal("w1", w1_raw[:], I32)
+        w1 = deal("w1", w1_raw[:], I32, P_W1)
         xq_scales = pick_scales("xq_scales", x_scale_table, offs_l)
         xq_words = pick_words("xq_words", x_table, offs_l)
         w1_s = deal("w1_s", w1_scales_raw[:], U8)
@@ -138,7 +162,7 @@ def tile_picked_jkeytwicehopphopb_none_po_kernel(
         for r in range(4):
             nc.sync.dma_start(key_scales[r:P:32, :].bitcast(I32), key_scales_dealt[8 * r : P : 32, :].bitcast(I32))
         w23_scales_raw = tile("w23_scales_raw", [P, N], U8, tag="key_scales_picked")
-        nc.gpsimd.memset(w23_scales_raw[:].bitcast(I32), 0)
+        nc.vector.memset(w23_scales_raw[:].bitcast(I32), 0)
         w2_raw = load_words("w2_raw", w2_words)
         w3_raw = load_words("w3_raw", w3_words)
         for k, src in ((0, w2_scales), (4, w3_scales)):
@@ -152,106 +176,117 @@ def tile_picked_jkeytwicehopphopb_none_po_kernel(
         n5_l = load_list("n5_l", n5)
         x2_scales = pick_scales("x2_scales", x_scale_table, two_l)
         x2_words = pick_words("x2_words", x_table, two_l)
-        keys_picked = pick_words("keys_picked", d_table, kidx_l)
+        keys_picked = pick_words("keys_picked", d_table, kidx_l, 4 * S * 19 + 2 * S)
         keys = deal("keys", keys_picked[:], I32)
         s_banks = [psum.tile([P, S], F32, name="s%d" % t, tag="bank%d" % (PACK + t)) for t in planes]
         for t in planes:
             mx(s_banks[t][:], keys, key_scales, t, x2_words[:], x2_scales[:], True, True)
 
-        z_planes = tile("z_planes", [P, PACK, S], BF16)
-        st = []
-
-        def z_second_hop(t):
-            far = tile("st_far%d" % t, [P, S], F32)
-            for lo, hi in HALVES:
-                fetch(t in V_N1B, far[:, lo:hi], st[t], n1_l, lo, hi)
-            nc.vector.scalar_tensor_tensor(z_planes[:, t, :], far[:], -0.5, st[t][:], ALU.mult, ALU.add)
-
-        for t in planes:
-            y = tile("y_sb%d" % t, [P, S], F32)
-            nc.scalar.activation(y[:], y_banks[t][:], ACT.Copy, scale=gn_t[:, t : t + 1])
-            far = tile("y_far%d" % t, [P, S], F32)
-            for lo, hi in HALVES:
-                fetch(t in V_N1A, far[:, lo:hi], y, n1_l, lo, hi)
-            st.append(reused.tile([P, S], F32, name="st%d" % t, offset=4 * S * t))
-            nc.vector.tensor_tensor(st[t][:], y[:], far[:], ALU.subtract)
-            if t >= LAG:
-                z_second_hop(t - LAG)
-
-        w2 = deal("w2", w2_raw[:], I32)
-        w3 = deal("w3", w3_raw[:], I32)
-        w23_s = deal("w23_s", w23_scales_raw[:], U8)
-
-        st2 = []
-        th = []
-        for t in planes:
-            s = tile("s_sb%d" % t, [P, S], F32)
-            nc.scalar.activation(s[:], s_banks[t][:], ACT.Copy, scale=0.0625)
-            far = tile("s_far%d" % t, [P, S], F32)
-            for lo, hi in HALVES:
-                fetch(t in V_N2, far[:, lo:hi], s, n2_l, lo, hi)
-            st2.append(tile("st2_%d" % t, [P, S], F32))
-            nc.vector.tensor_tensor(st2[t][:], s[:], far[:], ALU.add)
-            th.append(tile("tanh%d" % t, [P, S], F32))
-            nc.scalar.activation(th[t][:], st2[t][:], ACT.Tanh)
-            if t < LAG:
-                z_second_hop(PACK - LAG + t)
-
-        z_words = tile("z_words", [P, S], U32)
-        z_scales = tile("z_scales", [P, S], U8)
-        quantise("z_woven", z_planes, z_words[:], z_scales[:])
-
-        hs = [tile("h_sb%d" % t, [P, S], F32) for t in planes]
+        ys, y_far, st, st_far, ss, s_far, st2, th, got = {}, {}, {}, {}, {}, {}, {}, {}, {}
+        hs = [tile("h_sb%d" % t, [P, 704 if t == 1 else S + 8], F32) for t in planes]
         h_banks = [
             [psum.tile([P, hi - lo], F32, name="h%d_%d" % (c, t), tag="bank%d" % (PACK * c + t)) for t in planes]
-            for c, (lo, hi) in enumerate(Z2_CHUNKS)
+            for c, (lo, hi) in enumerate(HALVES)
         ]
-        lo, hi = Z2_CHUNKS[1]
-        for t in planes:
-            mx(h_banks[1][t][:], w2, w23_s, t, z_words[:, lo:hi], z_scales[:, lo:hi], True, False)
-        for c, (lo, hi) in enumerate(Z2_CHUNKS):
-            z2_planes = tile("z2_planes%d" % c, [P, PACK, hi - lo], BF16)
-            for t in planes:
-                far = tile("tanh_far%d_%d" % (c, t), [P, hi - lo], F32)
+        z2_planes = {}
+
+        def slot(name, n, width=S):
+            return reused.tile([P, width], F32, name=name, offset=4 * S * n)
+
+        def step(name, t, c):
+            if name == "ye":
+                ys[t] = slot("y_sb%d" % t, 40 + 2 * t, 2 * S)
+                nc.scalar.activation(ys[t][:, :S], y_banks[t][:], ACT.Copy, scale=gn_t[:, t : t + 1])
+            elif name == "yh":
+                y_far[t] = slot("y_far%d" % t, 3 if t in V_N1A else 25) if t >= 2 else tile("y_far%d" % t, [P, S], F32)
+                fetch(t in V_N1A, y_far[t][:], ys[t], n1_l, 0, S)
+            elif name == "sub":
+                if t in P_SUB:
+                    st[t] = slot("st%d" % t, 16 + 2 * t, 2 * S)
+                else:
+                    st[t] = slot("st%d" % t, t)
+                (nc.gpsimd if t in P_SUB else nc.vector).tensor_tensor(st[t][:, :S], ys[t][:, :S], y_far[t][:], ALU.subtract)
+            elif name == "zh":
+                st_far[t] = slot("st_far%d" % t, ZH[t]) if ZH[t] is not None else tile("st_far%d" % t, [P, S], F32)
+                fetch(t in V_N1B, st_far[t][:], st[t], n1_l, 0, S)
+            elif name == "zc":
+                if "zp" not in got:
+                    got["zp"] = reused.tile([P, PACK, S], BF16, name="z_planes", offset=4 * S * ZOFF)
+                z_planes = got["zp"]
+                nc.vector.scalar_tensor_tensor(z_planes[:, t, :], st_far[t][:], -0.5, st[t][:, :S], ALU.mult, ALU.add)
+            elif name == "se":
+                ss[t] = tile("s_sb%d" % t, [P, S + 8], F32)
+                nc.scalar.activation(ss[t][:, :S], s_banks[t][:], ACT.Copy, scale=0.0625)
+            elif name == "sh":
+                s_far[t] = slot("s_far%d" % t, 4 + t)
+                fetch(t in V_N2, s_far[t][:], ss[t], n2_l, 0, S)
+            elif name == "add":
+                st2[t] = slot("st2_%d" % t, t - 1) if t > 0 else tile("st2_%d" % t, [P, S], F32)
+                (nc.gpsimd if t in P_ADD else nc.vector).tensor_tensor(st2[t][:], ss[t][:, :S], s_far[t][:], ALU.add)
+            elif name == "th":
+                th[t] = tile("tanh%d" % t, [P, S], F32)
+                nc.scalar.activation(th[t][:], st2[t][:], ACT.Tanh)
+            elif name == "deal":
+                got["w2"] = deal("w2", w2_raw[:], I32, P_DEAL, 4 * S * 25 - 1536)
+                got["w3"] = deal("w3", w3_raw[:], I32, P_DEAL, 4 * S * 25 + 1024)
+                got["ws"] = deal("w23_s", w23_scales_raw[:], U8, P_DEAL, 4 * S * 25 + 512)
+            elif name == "zq":
+                got["zw"] = tile("z_words", [P, S], U32)
+                got["zs"] = tile("z_scales", [P, S], U8)
+                quantise("z_woven", got["zp"], got["zw"][:], got["zs"][:])
+                for cc, (lo, hi) in enumerate(HALVES):
+                    for tt in planes:
+                        mx(h_banks[cc][tt][:], got["w2"], got["ws"], tt, got["zw"][:, lo:hi], got["zs"][:, lo:hi], True, False)
+            elif name == "g3":
+                lo, hi = HALVES[c]
+                if t == 0:
+                    z2_planes[c] = reused.tile([P, PACK, HALF], BF16, name="z2_planes%d" % c, offset=4 * S * (ZOFF + c))
+                if c == 1 and HOLD3:
+                    if t == 0:
+                        got["late"] = reused.tile([P, PACK, HALF], F32, name="tanh_far_late", offset=4 * G + 4 * S * 2)
+                    far = got["late"][:, t, :]
+                else:
+                    far = tile("tanh_far%d_%d" % (c, t), [P, HALF], F32)
                 fetch((c, t) in V_N3, far[:], th[t], n3_l, lo, hi)
                 nc.vector.scalar_tensor_tensor(
-                    z2_planes[:, t, :], st2[t][:, lo:hi], gk_t[:, t : t + 1], far[:], ALU.mult, ALU.mult
+                    z2_planes[c][:, t, :], st2[t][:, lo:hi], gk_t[:, t : t + 1], far[:], ALU.mult, ALU.mult
                 )
-            z2_words = tile("z2_words%d" % c, [P, hi - lo], U32)
-            z2_scales = tile("z2_scales%d" % c, [P, hi - lo], U8)
-            quantise("z2_woven%d" % c, z2_planes, z2_words[:], z2_scales[:])
-            for t in planes:
-                if c == 1:
-                    mx(h_banks[c][t][:], w3, w23_s[4:P, :], t, z2_words[:], z2_scales[:], False, True)
-                else:
-                    for a, b in PIECES:
-                        mx(h_banks[c][t][:, a:b], w2, w23_s, t, z_words[:, a:b], z_scales[:, a:b], True, False)
-                        mx(h_banks[c][t][:, a:b], w3, w23_s[4:P, :], t, z2_words[:, a:b], z2_scales[:, a:b], False, True)
-        for c, (lo, hi) in enumerate(Z2_CHUNKS):
-            for t in planes:
-                if c == 1 and t % 2 == 1:
-                    nc.vector.tensor_copy(hs[t][:, lo:hi], h_banks[c][t][:])
-                else:
-                    nc.scalar.copy(hs[t][:, lo:hi], h_banks[c][t][:])
+            elif name == "z2q":
+                lo, hi = HALVES[c]
+                z2_words = tile("z2_words%d" % c, [P, HALF], U32)
+                z2_scales = tile("z2_scales%d" % c, [P, HALF], U8)
+                quantise("z2_woven%d" % c, z2_planes[c], z2_words[:], z2_scales[:])
+                for tt in planes:
+                    mx(h_banks[c][tt][:], got["w3"], got["ws"][4:P, :], tt, z2_words[:], z2_scales[:], False, True)
+                for tt in planes:
+                    if (c, tt) in V_EV:
+                        nc.vector.tensor_copy(hs[tt][:, lo:hi], h_banks[c][tt][:])
+                    else:
+                        nc.scalar.copy(hs[tt][:, lo:hi], h_banks[c][tt][:])
+
+        for word in ORDER.split():
+            name, t, c = (word.split(".") + ["0", "0"])[:3]
+            step(name, int(t), int(c))
 
         st3 = []
         for t in planes:
-            far = tile("h_far%d" % t, [P, S], F32)
-            for lo, hi in HALVES:
-                fetch(t in V_N4, far[:, lo:hi], hs[t], n4_l, lo, hi)
+            far = slot("h_far%d" % t, 30) if t == 3 else tile("h_far%d" % t, [P, S], F32)
+            for c, (lo, hi) in enumerate(HALVES if t == 3 else [(0, S)]):
+                fetch((c, t) in V_N4, far[:, lo:hi], hs[t], n4_l, lo, hi)
             st3.append(tile("st3_%d" % t, [P, S], F32))
-            nc.vector.tensor_tensor(st3[t][:], hs[t][:], far[:], ALU.max)
+            nc.vector.tensor_tensor(st3[t][:], hs[t][:, :S], far[:], ALU.max)
 
         out_rows = out_0.rearrange("(p t) j -> p t j", t=PACK)
         out_word_rows = out_1[0].rearrange("p n t -> p (n t)").bitcast(I32)
         out_scales = tile("out_scales", [P, S], U8)
         for c, (lo, hi) in enumerate(OUT_CHUNKS):
-            res = tile("res%d" % c, [P, PACK, hi - lo], F32)
+            res = reused.tile([P, PACK, hi - lo], F32, name="res0", offset=4 * S * 30 - 3072) if c == 0 else tile("res1", [P, PACK, hi - lo], F32)
+            late = reused.tile([P, PACK, hi - lo], F32, name="st3_far_late", offset=4 * S * 30 + 1024) if c == 1 and HOLD5 else None
             for t in planes:
-                far = tile("st3_far%d_%d" % (c, t), [P, hi - lo], F32)
+                far = late[:, t, :] if late is not None else tile("st3_far%d_%d" % (c, t), [P, hi - lo], F32)
                 fetch((c, t) in V_N5, far[:], st3[t], n5_l, lo, hi)
                 nc.vector.scalar_tensor_tensor(res[:, t, :], hs[t][:, lo:hi], -0.5, far[:], ALU.mult, ALU.add)
-            nc.sync.dma_start(out_rows[:, :, lo:hi], res[:])
+                nc.sync.dma_start(out_rows[:, t, lo:hi], res[:, t, :])
             out_words = tile("out_words%d" % c, [P, hi - lo], I32)
             quantise("out_woven%d" % c, res, out_words[:], out_scales[:, lo:hi])
             nc.sync.dma_start(out_word_rows[:, lo:hi], out_words[:])

@@ -20,29 +20,31 @@ PACK = 4
 HALF = S // 2
 LIST_COLS = S // 16
 HALVES = [(0, HALF), (HALF, S)]
-Z2_CHUNKS = [(0, 256), (256, S)]
+Z2_CHUNKS = [(0, 256), (256, 512)]
 OUT_CHUNKS = [(0, 256), (256, S)]
 PIECES = [(0, HALF)]
 P_SUB = (0, 1, 2, 3)
-P_ADD = ()
-P_DEAL = False
+P_ADD = (0, 1)
+P_DEAL = True
 P_RES = ()
-ZOFF = 45
+ZOFF = 4
 RING3 = 8
 RING5 = 8
 SOFF = 0
-ORDER = "ye.0 yh.0 sub.0 ye.1 yh.1 sub.1 ye.2 yh.2 sub.2 zh.0 ye.3 yh.3 sub.3 zh.1 zh.2 deal se.0 sh.0 add.0 zh.3 zc.0 se.1 sh.1 add.1 zc.1 se.2 sh.2 add.2 zc.2 se.3 sh.3 add.3 zc.3 th.0 th.1 th.2 th.3 zq g3.0.0 g3.1.0 g3.2.0 g3.3.0 z2q.0.0 g3.0.1 g3.1.1 g3.2.1 g3.3.1 z2q.0.1"
+ORDER = "ye.0 yh.0 sub.0 ye.1 yh.1 sub.1 zh.0 ye.2 yh.2 sub.2 ye.3 yh.3 sub.3 zh.1 zh.2 deal se.0 se.1 sh.0 add.0 zh.3 sh.1 add.1 se.2 sh.2 add.2 zc.0 se.3 sh.3 add.3 zc.1 zc.2 zc.3 ws zv zq th.0 th.1 th.2 th.3 g3.0.0 g3.1.0 g3.2.0 g3.3.0 g3.0.1 g3.1.1 z2q.0.0 g3.2.1 g3.3.1 z2q.0.1 ev.0.0 ev.0.1"
 HOLD3 = True
 HOLD5 = True
 SUBHOLD = 1
-P_W1 = False
-ZH = (0, 1, 2, None)
-V_EV = ((1, 1), (1, 3))
+P_W1 = True
+ZH = (3, None, None, None)
+V_EV = ((1, 1),)
+FAR3 = (4 * S * 38, 4 * S * 6, 0)
+WS = 4 * S * 35 + 1024
 LAG = 1
 V_N1A = (2,)
-V_N2 = ()
+V_N2 = (1,)
 V_N1B = (0, 1, 2, 3)
-V_N3 = ()
+V_N3 = ((1, 0),)
 V_N4 = ((0,1),(1,1),(0,3))
 V_N5 = ((0,0),)
 
@@ -143,6 +145,7 @@ def tile_picked_jkeytwicehopphopb_none_po_kernel(
         kidx_l = load_list("kidx_l", kidx)
         nc.sync.dma_start(d_scale_table[0:P:8, :].bitcast(I32), d_scales[0].bitcast(I32))
         gn_t = load_gain("gn_t", gn)
+        gk_t = load_gain("gk_t", gk)
         n1_l = load_list("n1_l", n1)
         two_l = load_list("two_l", two)
         d_table = reused.tile([P, G], I32, name="d_table", offset=0)
@@ -152,7 +155,7 @@ def tile_picked_jkeytwicehopphopb_none_po_kernel(
         w1 = deal("w1", w1_raw[:], I32, P_W1)
         xq_scales = pick_scales("xq_scales", x_scale_table, offs_l)
         xq_words = pick_words("xq_words", x_table, offs_l)
-        w1_s = deal("w1_s", w1_scales_raw[:], U8)
+        w1_s = deal("w1_s", w1_scales_raw[:], U8, P_W1)
         y_banks = [psum.tile([P, S], F32, name="y%d" % t, tag="bank%d" % t) for t in planes]
         for t in planes:
             mx(y_banks[t][:], w1, w1_s, t, xq_words[:], xq_scales[:], True, True)
@@ -170,7 +173,6 @@ def tile_picked_jkeytwicehopphopb_none_po_kernel(
                 nc.sync.dma_start(
                     w23_scales_raw[32 * q + k : 32 * q + k + 4, :].bitcast(I32), src[0, 4 * q : 4 * q + 4, :].bitcast(I32)
                 )
-        gk_t = load_gain("gk_t", gk)
         n3_l = load_list("n3_l", n3)
         n4_l = load_list("n4_l", n4)
         n5_l = load_list("n5_l", n5)
@@ -190,6 +192,13 @@ def tile_picked_jkeytwicehopphopb_none_po_kernel(
         ]
         z2_planes = {}
 
+        gk16 = tile("gk16", [P, PACK], F32)
+        nc.gpsimd.tensor_scalar(gk16[:], gk_t[:], 0.0625, 0.0, ALU.mult, ALU.add)
+        gk_zero = tile("gk_zero", [P, PACK], F32)
+        nc.gpsimd.tensor_scalar(gk_zero[:], gk_t[:], 0.0, None, ALU.is_equal)
+        gk_safe = tile("gk_safe", [P, PACK], F32)
+        nc.gpsimd.tensor_tensor(gk_safe[:], gk_t[:], gk_zero[:], ALU.add)
+
         def slot(name, n, width=S):
             return reused.tile([P, width], F32, name=name, offset=4 * S * n)
 
@@ -198,66 +207,78 @@ def tile_picked_jkeytwicehopphopb_none_po_kernel(
                 ys[t] = slot("y_sb%d" % t, 40 + 2 * t, 2 * S)
                 nc.scalar.activation(ys[t][:, :S], y_banks[t][:], ACT.Copy, scale=gn_t[:, t : t + 1])
             elif name == "yh":
-                y_far[t] = slot("y_far%d" % t, 3 if t in V_N1A else 25) if t >= 2 else tile("y_far%d" % t, [P, S], F32)
+                y_far[t] = got["st2"][:, 0, :] if t in V_N1A else slot("y_far%d" % t, 9 + t)
                 fetch(t in V_N1A, y_far[t][:], ys[t], n1_l, 0, S)
             elif name == "sub":
                 if t in P_SUB:
-                    st[t] = slot("st%d" % t, 16 + 2 * t, 2 * S)
+                    st[t] = slot("st%d" % t, 42 if t == 3 else 16 + 2 * t, 2 * S)
                 else:
                     st[t] = slot("st%d" % t, t)
                 (nc.gpsimd if t in P_SUB else nc.vector).tensor_tensor(st[t][:, :S], ys[t][:, :S], y_far[t][:], ALU.subtract)
             elif name == "zh":
-                st_far[t] = slot("st_far%d" % t, ZH[t]) if ZH[t] is not None else tile("st_far%d" % t, [P, S], F32)
+                if "st2" not in got:
+                    got["st2"] = reused.tile([P, PACK, S], F32, name="st2_all", offset=0)
+                st_far[t] = got["st2"][:, ZH[t], :] if ZH[t] is not None else tile("st_far%d" % t, [P, S], F32)
                 fetch(t in V_N1B, st_far[t][:], st[t], n1_l, 0, S)
             elif name == "zc":
                 if "zp" not in got:
-                    got["zp"] = reused.tile([P, PACK, S], BF16, name="z_planes", offset=4 * S * ZOFF)
+                    got["zp"] = reused.tile([P, PACK, S], BF16, name="z_planes", offset=4 * S * 35 - 3072)
                 z_planes = got["zp"]
                 nc.vector.scalar_tensor_tensor(z_planes[:, t, :], st_far[t][:], -0.5, st[t][:, :S], ALU.mult, ALU.add)
             elif name == "se":
-                ss[t] = tile("s_sb%d" % t, [P, S + 8], F32)
-                nc.scalar.activation(ss[t][:, :S], s_banks[t][:], ACT.Copy, scale=0.0625)
+                ss[t] = slot("s_sb1", 35, 704) if t == 1 else tile("s_sb%d" % t, [P, S + 8], F32)
+                nc.scalar.activation(ss[t][:, :S], s_banks[t][:], ACT.Copy, scale=gk16[:, t : t + 1])
             elif name == "sh":
-                s_far[t] = slot("s_far%d" % t, 4 + t)
+                s_far[t] = got["st2"][:, 2, :] if t == 1 else slot("s_far%d" % t, 4 + t)
                 fetch(t in V_N2, s_far[t][:], ss[t], n2_l, 0, S)
             elif name == "add":
-                st2[t] = slot("st2_%d" % t, t - 1) if t > 0 else tile("st2_%d" % t, [P, S], F32)
+                st2[t] = got["st2"][:, t, :]
                 (nc.gpsimd if t in P_ADD else nc.vector).tensor_tensor(st2[t][:], ss[t][:, :S], s_far[t][:], ALU.add)
             elif name == "th":
                 th[t] = tile("tanh%d" % t, [P, S], F32)
-                nc.scalar.activation(th[t][:], st2[t][:], ACT.Tanh)
+                nc.scalar.activation(th[t][:], st2[t][:], ACT.Tanh, scale=got["inv"][:, t : t + 1])
             elif name == "deal":
-                got["w2"] = deal("w2", w2_raw[:], I32, P_DEAL, 4 * S * 25 - 1536)
-                got["w3"] = deal("w3", w3_raw[:], I32, P_DEAL, 4 * S * 25 + 1024)
-                got["ws"] = deal("w23_s", w23_scales_raw[:], U8, P_DEAL, 4 * S * 25 + 512)
+                got["w2"] = deal("w2", w2_raw[:], I32, P_DEAL)
+                got["inv"] = reused.tile([P, PACK], F32, name="inv_gk", offset=4 * S * 10)
+                nc.vector.reciprocal(got["inv"][:], gk_safe[:])
+            elif name == "ws":
+                got["w3"] = deal("w3", w3_raw[:], I32, False, 4 * S * 35 + 1536)
+                got["ws"] = deal("w23_s", w23_scales_raw[:], U8, False, WS)
+            elif name == "zv":
+                got["zv"] = tile("z_woven", [P, S, PACK], BF16)
+                nc.vector.tensor_copy(
+                    got["zv"][:].rearrange("p (c i) t -> p c t i", i=4), got["zp"][:].rearrange("p t (c i) -> p c t i", i=4)
+                )
             elif name == "zq":
                 got["zw"] = tile("z_words", [P, S], U32)
                 got["zs"] = tile("z_scales", [P, S], U8)
-                quantise("z_woven", got["zp"], got["zw"][:], got["zs"][:])
+                nc.vector.quantize_mx(got["zw"][:].bitcast(FP8X4), got["zs"][:], got["zv"][:].rearrange("p j t -> p (j t)"))
                 for cc, (lo, hi) in enumerate(HALVES):
                     for tt in planes:
                         mx(h_banks[cc][tt][:], got["w2"], got["ws"], tt, got["zw"][:, lo:hi], got["zs"][:, lo:hi], True, False)
             elif name == "g3":
-                lo, hi = HALVES[c]
+                lo, hi = Z2_CHUNKS[c]
                 if t == 0:
-                    z2_planes[c] = reused.tile([P, PACK, HALF], BF16, name="z2_planes%d" % c, offset=4 * S * (ZOFF + c))
-                if c == 1 and HOLD3:
-                    if t == 0:
-                        got["late"] = reused.tile([P, PACK, HALF], F32, name="tanh_far_late", offset=4 * G + 4 * S * 2)
-                    far = got["late"][:, t, :]
-                else:
-                    far = tile("tanh_far%d_%d" % (c, t), [P, HALF], F32)
-                fetch((c, t) in V_N3, far[:], th[t], n3_l, lo, hi)
-                nc.vector.scalar_tensor_tensor(
-                    z2_planes[c][:, t, :], st2[t][:, lo:hi], gk_t[:, t : t + 1], far[:], ALU.mult, ALU.mult
-                )
+                    z2_planes[c] = reused.tile([P, PACK, hi - lo], F32, name="tanh_far%d" % c, offset=FAR3[c])
+                fetch((c, t) in V_N3, z2_planes[c][:, t, :], th[t], n3_l, lo, hi)
             elif name == "z2q":
-                lo, hi = HALVES[c]
-                z2_words = tile("z2_words%d" % c, [P, HALF], U32)
-                z2_scales = tile("z2_scales%d" % c, [P, HALF], U8)
-                quantise("z2_woven%d" % c, z2_planes[c], z2_words[:], z2_scales[:])
+                lo, hi = Z2_CHUNKS[c]
+                half = lo // HALF
+                z2_words = tile("z2_words%d" % c, [P, hi - lo], U32)
+                z2_scales = tile("z2_scales%d" % c, [P, hi - lo], U8)
+                woven = tile("z2_woven%d" % c, [P, hi - lo, PACK], BF16)
+                nc.vector.tensor_tensor(
+                    woven[:].rearrange("p (c i) t -> p c t i", i=4),
+                    got["st2"][:, :, lo:hi].rearrange("p t (c i) -> p c t i", i=4),
+                    z2_planes[c][:].rearrange("p t (c i) -> p c t i", i=4),
+                    ALU.mult,
+                )
+                nc.vector.quantize_mx(z2_words[:].bitcast(FP8X4), z2_scales[:], woven[:].rearrange("p j t -> p (j t)"))
+                last = hi % HALF == 0
                 for tt in planes:
-                    mx(h_banks[c][tt][:], got["w3"], got["ws"][4:P, :], tt, z2_words[:], z2_scales[:], False, True)
+                    mx(h_banks[half][tt][:, lo - half * HALF : hi - half * HALF], got["w3"], got["ws"][4:P, :], tt, z2_words[:], z2_scales[:], False, last)
+            elif name == "ev":
+                lo, hi = HALVES[c]
                 for tt in planes:
                     if (c, tt) in V_EV:
                         nc.vector.tensor_copy(hs[tt][:, lo:hi], h_banks[c][tt][:])

from contextlib import ExitStack

import concourse.mybir as mybir

K, T, S, N, H, G = 512, 1024, 512, 512, 512, 2048
FLOPS = 4 * 2 * 512 * 512 * 512

F32 = mybir.dt.float32
BF16 = mybir.dt.bfloat16
I32 = mybir.dt.int32
U32 = mybir.dt.uint32
U16 = mybir.dt.uint16
U8 = mybir.dt.uint8
FP8X4 = mybir.dt.float8_e4m3fn_x4
ALU = mybir.AluOpType
ACT = mybir.ActivationFunctionType

P = 128
PACK = 4
HALF = S // 2
LIST_COLS = S // 16
HALVES = [(0, HALF), (HALF, S)]
Z2_CHUNKS = [(0, 256), (256, 512)]
OUT_CHUNKS = [(0, 256), (256, S)]
PIECES = [(0, HALF)]
P_SUB = (0, 1, 2, 3)
P_ADD = (0, 1)
P_DEAL = True
P_RES = ()
ZOFF = 4
RING3 = 8
RING5 = 8
SOFF = 0
ORDER = "ye.0 yh.0 sub.0 ye.1 yh.1 sub.1 zh.0 ye.2 yh.2 sub.2 ye.3 yh.3 sub.3 zh.1 zh.2 deal se.0 se.1 sh.0 add.0 zh.3 sh.1 add.1 se.2 sh.2 add.2 zc.0 se.3 sh.3 add.3 zc.1 zc.2 zc.3 ws zv zq th.0 th.1 th.2 th.3 g3.0.0 g3.1.0 g3.2.0 g3.3.0 g3.0.1 g3.1.1 z2q.0.0 g3.2.1 g3.3.1 z2q.0.1 ev.0.0 ev.0.1"
HOLD3 = True
HOLD5 = True
SUBHOLD = 1
P_W1 = True
ZH = (3, None, None, None)
V_EV = ((1, 1),)
FAR3 = (4 * S * 38, 4 * S * 6, 0)
WS = 4 * S * 35 + 1024
LAG = 1
V_N1A = (2,)
V_N2 = (1,)
V_N1B = (0, 1, 2, 3)
V_N3 = ((1, 0),)
V_N4 = ((0,1),(1,1),(0,3))
V_N5 = ((0,0),)


def tile_picked_jkeytwicehopphopb_none_po_kernel(
    tc, x_words, x_scales, w1_words, w1_scales, d_words, d_scales, gn, gk, w2_words, w2_scales, w3_words, w3_scales,
    offs, kidx, two, n1, n2, n3, n4, n5, out_0, out_1, out_2,
):
    nc = tc.nc
    planes = range(PACK)

    with ExitStack() as ctx:
        lists = ctx.enter_context(tc.tile_pool(name="lists", bufs=1))
        sb = ctx.enter_context(tc.tile_pool(name="sb", bufs=1))
        reused = ctx.enter_context(tc.tile_pool(name="reused", bufs=1))
        psum = ctx.enter_context(tc.psum_pool(name="psum", bufs=1))

        def tile(name, shape, dtype, tag=None):
            return sb.tile(shape, dtype, name=name, tag=tag or name, align_bytes=64)

        def load_list(name, src):
            dst = lists.tile([P, LIST_COLS], U16, name=name)
            nc.sync.dma_start(dst[:], src)
            return dst

        def load_words(name, src):
            dst = tile(name, [P, src.shape[2]], I32)
            nc.sync.dma_start(dst[:], src[0].rearrange("p n t -> p (n t)").bitcast(I32))
            return dst

        def load_scales_repeated(name, src):
            dst = tile(name, [P, src.shape[2]], U8)
            for q in range(4):
                rows = src[0, 4 * q : 4 * q + 4, :].bitcast(I32).rearrange("r c -> (r c)")
                nc.sync.dma_start(dst[32 * q : 32 * q + 32, :].bitcast(I32), rows.partition_broadcast(8))
            return dst

        def load_gain(name, src):
            dst = tile(name, [P, PACK], F32)
            nc.sync.dma_start(dst[:], src.rearrange("(p t) o -> p (t o)", t=PACK))
            return dst

        def deal(name, src, dtype, on_pool=False, offset=None):
            if offset is None:
                dst = tile(name, [P, 512], dtype)
            else:
                dst = reused.tile([P, 512], dtype, name=name, offset=offset, align_bytes=64)
            if on_pool:
                nc.gpsimd.tensor_copy(dst[:].rearrange("p (t m) -> p t m", t=PACK), src.rearrange("p (m t) -> p t m", t=PACK))
                return dst
            nc.vector.tensor_copy(dst[:].rearrange("p (t m) -> p m t", t=PACK), src.rearrange("p (m t) -> p m t", t=PACK))
            return dst

        def pick_words(name, table, offsets, offset=None):
            if offset is None:
                dst = tile(name, [P, 512], I32)
            else:
                dst = reused.tile([P, 512], I32, name=name, offset=offset)
            nc.vector.tensor_copy(dst[:].bitcast(U32), table[:].bitcast(U32).indirect(offsets[:]))
            return dst

        def pick_scales(name, table, offsets):
            dst = tile(name, [P, 512], U8)
            nc.vector.tensor_copy(dst[:], table[:].indirect(offsets[:]))
            return dst

        def fetch(on_vector, dst, window, offsets, lo, hi):
            looked_up = window[:].indirect(offsets[:, lo // 16 : hi // 16])
            if on_vector:
                nc.vector.tensor_copy(dst, looked_up)
            else:
                nc.scalar.activation(dst, looked_up, ACT.Copy)

        def mx(out, w_words, w_scales, t, a_words, a_scales, start, stop):
            m = slice(t * P, (t + 1) * P)
            nc.tensor.matmul_mx(
                out, lhsT=w_words[:, m].bitcast(FP8X4), lhsT_scale=w_scales[:, m],
                rhs=a_words.bitcast(FP8X4), rhs_scale=a_scales, start=start, stop=stop,
            )

        def quantise(name, src, words, scales):
            woven = tile(name, [P, src.shape[2], PACK], BF16)
            nc.vector.tensor_copy(
                woven[:].rearrange("p (c i) t -> p c t i", i=4), src[:].rearrange("p t (c i) -> p c t i", i=4)
            )
            nc.vector.quantize_mx(words.bitcast(FP8X4), scales, woven[:].rearrange("p j t -> p (j t)"))

        d_scale_table = tile("d_scale_table", [P, G], U8)
        nc.gpsimd.memset(d_scale_table[:].bitcast(I32), 0)
        key_scales = tile("key_scales", [P, H], U8)
        nc.gpsimd.memset(key_scales[:].bitcast(I32), 0)

        offs_l = load_list("offs_l", offs)
        x_scale_table = load_scales_repeated("x_scale_table", x_scales)
        x_table = load_words("x_table", x_words)
        w1_raw = load_words("w1_raw", w1_words)
        w1_scales_raw = load_scales_repeated("w1_scales_raw", w1_scales)
        kidx_l = load_list("kidx_l", kidx)
        nc.sync.dma_start(d_scale_table[0:P:8, :].bitcast(I32), d_scales[0].bitcast(I32))
        gn_t = load_gain("gn_t", gn)
        gk_t = load_gain("gk_t", gk)
        n1_l = load_list("n1_l", n1)
        two_l = load_list("two_l", two)
        d_table = reused.tile([P, G], I32, name="d_table", offset=0)
        nc.sync.dma_start(d_table[:], d_words[0].rearrange("p n t -> p (n t)").bitcast(I32))
        n2_l = load_list("n2_l", n2)

        w1 = deal("w1", w1_raw[:], I32, P_W1)
        xq_scales = pick_scales("xq_scales", x_scale_table, offs_l)
        xq_words = pick_words("xq_words", x_table, offs_l)
        w1_s = deal("w1_s", w1_scales_raw[:], U8, P_W1)
        y_banks = [psum.tile([P, S], F32, name="y%d" % t, tag="bank%d" % t) for t in planes]
        for t in planes:
            mx(y_banks[t][:], w1, w1_s, t, xq_words[:], xq_scales[:], True, True)

        key_scales_picked = pick_scales("key_scales_picked", d_scale_table, kidx_l)
        key_scales_dealt = deal("key_scales_dealt", key_scales_picked[:], U8)
        for r in range(4):
            nc.sync.dma_start(key_scales[r:P:32, :].bitcast(I32), key_scales_dealt[8 * r : P : 32, :].bitcast(I32))
        w23_scales_raw = tile("w23_scales_raw", [P, N], U8, tag="key_scales_picked")
        nc.vector.memset(w23_scales_raw[:].bitcast(I32), 0)
        w2_raw = load_words("w2_raw", w2_words)
        w3_raw = load_words("w3_raw", w3_words)
        for k, src in ((0, w2_scales), (4, w3_scales)):
            for q in range(4):
                nc.sync.dma_start(
                    w23_scales_raw[32 * q + k : 32 * q + k + 4, :].bitcast(I32), src[0, 4 * q : 4 * q + 4, :].bitcast(I32)
                )
        n3_l = load_list("n3_l", n3)
        n4_l = load_list("n4_l", n4)
        n5_l = load_list("n5_l", n5)
        x2_scales = pick_scales("x2_scales", x_scale_table, two_l)
        x2_words = pick_words("x2_words", x_table, two_l)
        keys_picked = pick_words("keys_picked", d_table, kidx_l, 4 * S * 19 + 2 * S)
        keys = deal("keys", keys_picked[:], I32)
        s_banks = [psum.tile([P, S], F32, name="s%d" % t, tag="bank%d" % (PACK + t)) for t in planes]
        for t in planes:
            mx(s_banks[t][:], keys, key_scales, t, x2_words[:], x2_scales[:], True, True)

        ys, y_far, st, st_far, ss, s_far, st2, th, got = {}, {}, {}, {}, {}, {}, {}, {}, {}
        hs = [tile("h_sb%d" % t, [P, 704 if t == 1 else S + 8], F32) for t in planes]
        h_banks = [
            [psum.tile([P, hi - lo], F32, name="h%d_%d" % (c, t), tag="bank%d" % (PACK * c + t)) for t in planes]
            for c, (lo, hi) in enumerate(HALVES)
        ]
        z2_planes = {}

        gk16 = tile("gk16", [P, PACK], F32)
        nc.gpsimd.tensor_scalar(gk16[:], gk_t[:], 0.0625, 0.0, ALU.mult, ALU.add)
        gk_zero = tile("gk_zero", [P, PACK], F32)
        nc.gpsimd.tensor_scalar(gk_zero[:], gk_t[:], 0.0, None, ALU.is_equal)
        gk_safe = tile("gk_safe", [P, PACK], F32)
        nc.gpsimd.tensor_tensor(gk_safe[:], gk_t[:], gk_zero[:], ALU.add)

        def slot(name, n, width=S):
            return reused.tile([P, width], F32, name=name, offset=4 * S * n)

        def step(name, t, c):
            if name == "ye":
                ys[t] = slot("y_sb%d" % t, 40 + 2 * t, 2 * S)
                nc.scalar.activation(ys[t][:, :S], y_banks[t][:], ACT.Copy, scale=gn_t[:, t : t + 1])
            elif name == "yh":
                y_far[t] = got["st2"][:, 0, :] if t in V_N1A else slot("y_far%d" % t, 9 + t)
                fetch(t in V_N1A, y_far[t][:], ys[t], n1_l, 0, S)
            elif name == "sub":
                if t in P_SUB:
                    st[t] = slot("st%d" % t, 42 if t == 3 else 16 + 2 * t, 2 * S)
                else:
                    st[t] = slot("st%d" % t, t)
                (nc.gpsimd if t in P_SUB else nc.vector).tensor_tensor(st[t][:, :S], ys[t][:, :S], y_far[t][:], ALU.subtract)
            elif name == "zh":
                if "st2" not in got:
                    got["st2"] = reused.tile([P, PACK, S], F32, name="st2_all", offset=0)
                st_far[t] = got["st2"][:, ZH[t], :] if ZH[t] is not None else tile("st_far%d" % t, [P, S], F32)
                fetch(t in V_N1B, st_far[t][:], st[t], n1_l, 0, S)
            elif name == "zc":
                if "zp" not in got:
                    got["zp"] = reused.tile([P, PACK, S], BF16, name="z_planes", offset=4 * S * 35 - 3072)
                z_planes = got["zp"]
                nc.vector.scalar_tensor_tensor(z_planes[:, t, :], st_far[t][:], -0.5, st[t][:, :S], ALU.mult, ALU.add)
            elif name == "se":
                ss[t] = slot("s_sb1", 35, 704) if t == 1 else tile("s_sb%d" % t, [P, S + 8], F32)
                nc.scalar.activation(ss[t][:, :S], s_banks[t][:], ACT.Copy, scale=gk16[:, t : t + 1])
            elif name == "sh":
                s_far[t] = got["st2"][:, 2, :] if t == 1 else slot("s_far%d" % t, 4 + t)
                fetch(t in V_N2, s_far[t][:], ss[t], n2_l, 0, S)
            elif name == "add":
                st2[t] = got["st2"][:, t, :]
                (nc.gpsimd if t in P_ADD else nc.vector).tensor_tensor(st2[t][:], ss[t][:, :S], s_far[t][:], ALU.add)
            elif name == "th":
                th[t] = tile("tanh%d" % t, [P, S], F32)
                nc.scalar.activation(th[t][:], st2[t][:], ACT.Tanh, scale=got["inv"][:, t : t + 1])
            elif name == "deal":
                got["w2"] = deal("w2", w2_raw[:], I32, P_DEAL)
                got["inv"] = reused.tile([P, PACK], F32, name="inv_gk", offset=4 * S * 10)
                nc.vector.reciprocal(got["inv"][:], gk_safe[:])
            elif name == "ws":
                got["w3"] = deal("w3", w3_raw[:], I32, False, 4 * S * 35 + 1536)
                got["ws"] = deal("w23_s", w23_scales_raw[:], U8, False, WS)
            elif name == "zv":
                got["zv"] = tile("z_woven", [P, S, PACK], BF16)
                nc.vector.tensor_copy(
                    got["zv"][:].rearrange("p (c i) t -> p c t i", i=4), got["zp"][:].rearrange("p t (c i) -> p c t i", i=4)
                )
            elif name == "zq":
                got["zw"] = tile("z_words", [P, S], U32)
                got["zs"] = tile("z_scales", [P, S], U8)
                nc.vector.quantize_mx(got["zw"][:].bitcast(FP8X4), got["zs"][:], got["zv"][:].rearrange("p j t -> p (j t)"))
                for cc, (lo, hi) in enumerate(HALVES):
                    for tt in planes:
                        mx(h_banks[cc][tt][:], got["w2"], got["ws"], tt, got["zw"][:, lo:hi], got["zs"][:, lo:hi], True, False)
            elif name == "g3":
                lo, hi = Z2_CHUNKS[c]
                if t == 0:
                    z2_planes[c] = reused.tile([P, PACK, hi - lo], F32, name="tanh_far%d" % c, offset=FAR3[c])
                fetch((c, t) in V_N3, z2_planes[c][:, t, :], th[t], n3_l, lo, hi)
            elif name == "z2q":
                lo, hi = Z2_CHUNKS[c]
                half = lo // HALF
                z2_words = tile("z2_words%d" % c, [P, hi - lo], U32)
                z2_scales = tile("z2_scales%d" % c, [P, hi - lo], U8)
                woven = tile("z2_woven%d" % c, [P, hi - lo, PACK], BF16)
                nc.vector.tensor_tensor(
                    woven[:].rearrange("p (c i) t -> p c t i", i=4),
                    got["st2"][:, :, lo:hi].rearrange("p t (c i) -> p c t i", i=4),
                    z2_planes[c][:].rearrange("p t (c i) -> p c t i", i=4),
                    ALU.mult,
                )
                nc.vector.quantize_mx(z2_words[:].bitcast(FP8X4), z2_scales[:], woven[:].rearrange("p j t -> p (j t)"))
                last = hi % HALF == 0
                for tt in planes:
                    mx(h_banks[half][tt][:, lo - half * HALF : hi - half * HALF], got["w3"], got["ws"][4:P, :], tt, z2_words[:], z2_scales[:], False, last)
            elif name == "ev":
                lo, hi = HALVES[c]
                for tt in planes:
                    if (c, tt) in V_EV:
                        nc.vector.tensor_copy(hs[tt][:, lo:hi], h_banks[c][tt][:])
                    else:
                        nc.scalar.copy(hs[tt][:, lo:hi], h_banks[c][tt][:])

        for word in ORDER.split():
            name, t, c = (word.split(".") + ["0", "0"])[:3]
            step(name, int(t), int(c))

        st3 = []
        for t in planes:
            far = slot("h_far%d" % t, 30) if t == 3 else tile("h_far%d" % t, [P, S], F32)
            for c, (lo, hi) in enumerate(HALVES if t == 3 else [(0, S)]):
                fetch((c, t) in V_N4, far[:, lo:hi], hs[t], n4_l, lo, hi)
            st3.append(tile("st3_%d" % t, [P, S], F32))
            nc.vector.tensor_tensor(st3[t][:], hs[t][:, :S], far[:], ALU.max)

        out_rows = out_0.rearrange("(p t) j -> p t j", t=PACK)
        out_word_rows = out_1[0].rearrange("p n t -> p (n t)").bitcast(I32)
        out_scales = tile("out_scales", [P, S], U8)
        for c, (lo, hi) in enumerate(OUT_CHUNKS):
            res = reused.tile([P, PACK, hi - lo], F32, name="res0", offset=4 * S * 30 - 3072) if c == 0 else tile("res1", [P, PACK, hi - lo], F32)
            late = reused.tile([P, PACK, hi - lo], F32, name="st3_far_late", offset=4 * S * 30 + 1024) if c == 1 and HOLD5 else None
            for t in planes:
                far = late[:, t, :] if late is not None else tile("st3_far%d_%d" % (c, t), [P, hi - lo], F32)
                fetch((c, t) in V_N5, far[:], st3[t], n5_l, lo, hi)
                nc.vector.scalar_tensor_tensor(res[:, t, :], hs[t][:, lo:hi], -0.5, far[:], ALU.mult, ALU.add)
                nc.sync.dma_start(out_rows[:, t, lo:hi], res[:, t, :])
            out_words = tile("out_words%d" % c, [P, hi - lo], I32)
            quantise("out_woven%d" % c, res, out_words[:], out_scales[:, lo:hi])
            nc.sync.dma_start(out_word_rows[:, lo:hi], out_words[:])
        for q in range(4):
            queue = nc.scalar if q % 2 else nc.sync
            queue.dma_start(out_2[0, 4 * q : 4 * q + 4, :].bitcast(I32), out_scales[32 * q : 32 * q + 4, :].bitcast(I32))
